import numpy as np
CORES = [8,11,14,16,19,22,24,27,30]
N = 9
TK = 1024
NT = N * TK
EPS = 0.01
def setup_inputs(rng):
    x = (rng.standard_normal((N, 128, TK), dtype=np.float32) * (0.5 + np.arange(N, dtype=np.float32).reshape(N, 1, 1) / N) + rng.standard_normal((N, 128, 1), dtype=np.float32))
    return {"x": x}
def setup_inputs_big(rng):
    d = setup_inputs(rng)
    for k in ("x",): d[k] = (d[k].astype(np.float32) * 1024.0).astype(d[k].dtype)
    return d
def setup_inputs_small(rng):
    d = setup_inputs(rng)
    for k in ("x",): d[k] = (d[k].astype(np.float32) * (1 / 1024.0)).astype(d[k].dtype)
    return d
def setup_inputs_apart(rng):
    d = setup_inputs(rng)
    f = (10.0 ** rng.permutation(np.linspace(-1.5, 1.5, N))).astype(np.float32).reshape(N, 1, 1)
    for k in ("x",): d[k] = (d[k].astype(np.float32) * f).astype(d[k].dtype)
    return d
def setup_inputs_mixed(rng):
    d = setup_inputs(rng)
    f = (10.0 ** rng.uniform(-3, 3, (1, 128, 1))).astype(np.float32); shape = rng.integers(3, size=(1, 128, 1))
    for k in ("x",):
        x = d[k].astype(np.float32)
        m = x.mean(axis=(0, 2), keepdims=True); level = m + np.sign(x - m) * np.abs(x - m).mean(axis=(0, 2), keepdims=True) * rng.uniform(0.9, 1.1, x.shape).astype(np.float32)
        other = x * np.where(rng.random(x.shape) < 0.5, 0.1, 1.0).astype(np.float32)
        d[k] = (np.where(shape == 1, level, np.where(shape == 2, other, x)) * f).astype(d[k].dtype)
    return d
def setup_inputs_offset(rng):
    d = setup_inputs(rng)
    x = d["x"]; spread = x.std(axis=(0, 2), keepdims=True)
    d["x"] = (x + spread * rng.uniform(16, 48, (1, 128, 1)) * rng.choice([-1.0, 1.0], (1, 128, 1))).astype(np.float32)
    return d
def reference(x):
    X = x.astype(np.float64)
    mu = X.sum(axis=(0, 2)).reshape(1, 128, 1) / NT
    rs = 1.0 / np.sqrt(((X - mu) ** 2).sum(axis=(0, 2)).reshape(1, 128, 1) / NT + EPS)
    n = (X - mu) * rs
    return {"y": n.astype(np.float32)}

@@ -1,0 +1,177 @@
+from concourse.bass import DstId, RemoteDMATransfer
+from concourse.mybir import AluOpType, AxisListType, ActivationFunctionType
+
+NR = 9
+TK = 1024
+NT = NR * TK
+EPS = 0.01
+SUB = 128
+NS = TK // SUB
+KT = NR * NS
+SLOT = 2 * NS
+LOADS = [(0, 512), (512, 1024)]
+STORES = [((0, 128), (128, 256)), ((256, 640), (640, 1024))]
+
+SCRATCH = {
+    "xs": ("sbuf", [128, TK], "float32"),
+    "ys": ("sbuf", [128, TK], "float32"),
+    "sq": ("sbuf", [128, TK], "float32"),
+    "land": ("sbuf", [128, NR * SLOT], "float32"),
+    "j1": ("sbuf", [128, KT], "float32"),
+    "j2": ("sbuf", [128, KT], "float32"),
+    "s0": ("sbuf", [128, 4], "float32"),
+    "hh": ("sbuf", [128, 4], "float32"),
+    "kk": ("sbuf", [128, 4], "float32"),
+    "r1": ("sbuf", [128, 4], "float32"),
+    "ww": ("sbuf", [128, 4], "float32"),
+    "qq": ("sbuf", [128, 4], "float32"),
+    "w2": ("sbuf", [128, 4], "float32"),
+    "mu": ("sbuf", [128, 4], "float32"),
+    "tt": ("sbuf", [128, 4], "float32"),
+    "rt": ("sbuf", [128, 4], "float32"),
+    "rn": ("sbuf", [128, 4], "float32"),
+}
+SEMAPHORES = (["ld%d" % i for i in range(len(LOADS))] + ["a%d" % j for j in range(NS)]
+              + ["b1s", "b2s", "peer", "far", "sent", "es0", "eis", "ek", "er1", "ew", "eq", "ew2", "emu", "et",
+                 "ert", "ers", "st"]
+              + ["nv%d" % i for i in range(len(STORES))] + ["ns%d" % i for i in range(len(STORES))])
+
+
+def _bits(m):
+    return bin(m).count("1")
+
+
+def _plan(cores, topo):
+    chips = []
+    for c in cores:
+        if topo.chip(c) not in chips:
+            chips.append(topo.chip(c))
+    groups = [[c for c in cores if topo.chip(c) == ch] for ch in chips]
+    slot = {}
+    for grp in groups:
+        for c in grp:
+            slot[c] = len(slot)
+    serve = {c: [] for c in cores}
+    for grp in groups:
+        dests = [d for d in cores if d not in grp]
+        can = {d: [s for s in grp if topo.may_write(s, d)] for d in dests}
+        for d in sorted(dests, key=lambda d: (len(can[d]), slot[d])):
+            s = min(can[d], key=lambda s: (len(serve[s]), 0 if topo.die(s) == topo.die(d) else 1, slot[s]))
+            serve[s].append(d)
+    return groups, slot, serve
+
+
+def _mask(core, dests, topo):
+    m = topo.mask(core, dests[0])
+    for d in dests[1:]:
+        m &= topo.mask(core, d)
+    return m
+
+
+def _send(g, T, topo, core, dests, lo, hi, sem):
+    m = _mask(core, dests, topo)
+    ids = [DstId(rid=topo.addr(d)[0], pnc=topo.addr(d)[1]) for d in dests]
+    g.remote_dma_fused([RemoteDMATransfer(dst_ids=ids, dma_engine_mask=m, remote_sem=sem,
+                                          srcs=[T.land[:, lo:hi]], dsts=[T.land[:, lo:hi] for d in dests],
+                                          alu_op=0)], local_sem=T.sem.sent)
+    return _bits(m)
+
+
+def rank_program(g, core, T, topo):
+    if T.rank_of(core) is None:
+        return
+    V, S, Y = g.vector, g.scalar, g.sync
+    sem = T.sem
+    A = ActivationFunctionType
+    mult, add, sub = AluOpType.mult, AluOpType.add, AluOpType.subtract
+    groups, slot, serve = _plan(list(T.cores), topo)
+    mine = [grp for grp in groups if core in grp][0]
+    peers = [c for c in mine if c != core]
+    own = slot[core] * SLOT
+    blk_lo, blk_hi = slot[mine[0]] * SLOT, (slot[mine[-1]] + 1) * SLOT
+    n_peer = sum(2 * _bits(_mask(p, [c for c in mine if c != p], topo)) for p in peers)
+    n_far = sum(_bits(_mask(s, serve[s], topo)) for s in T.cores if core in serve[s])
+
+    def col(t, i=0):
+        return t[:, i:i + 1]
+
+    for i, (lo, hi) in enumerate(LOADS):
+        (Y if i % 2 == 0 else S).dma_start(T.xs[:, lo:hi], T.x[:, lo:hi]).then_inc(sem["ld%d" % i], 16)
+
+    seen_v, seen_s = -1, -1
+    for j in range(NS):
+        lo, hi = j * SUB, (j + 1) * SUB
+        blk = [i for i, (a, b) in enumerate(LOADS) if a <= lo and hi <= b][0]
+        if blk != seen_v:
+            V.wait_ge(sem["ld%d" % blk], 16)
+            seen_v = blk
+        V.tensor_reduce(col(T.land, own + 2 * j), T.xs[:, lo:hi], AxisListType.X, add,
+                        negate=True).then_inc(sem["a%d" % j], 1)
+    for j in range(NS):
+        lo, hi = j * SUB, (j + 1) * SUB
+        blk = [i for i, (a, b) in enumerate(LOADS) if a <= lo and hi <= b][0]
+        if blk != seen_s:
+            S.wait_ge(sem["ld%d" % blk], 16)
+            seen_s = blk
+        S.wait_ge(sem["a%d" % j], 1)
+        S.activation(T.sq[:, lo:hi], T.xs[:, lo:hi], A.Square, bias=col(T.land, own + 2 * j), scale=float(SUB),
+                     accum_out=col(T.land, own + 2 * j + 1)).then_inc(sem.b1s if j == 0 else sem.b2s, 1)
+
+    n_sent = 0
+    g.wait_ge(sem.a0, 1)
+    g.wait_ge(sem.b1s, 1)
+    n_sent += _send(g, T, topo, core, peers, own, own + 2, sem.peer)
+    g.wait_ge(sem.b2s, NS - 1)
+    n_sent += _send(g, T, topo, core, peers, own + 2, own + SLOT, sem.peer)
+    g.wait_ge(sem.peer, n_peer)
+    if serve[core]:
+        n_sent += _send(g, T, topo, core, serve[core], blk_lo, blk_hi, sem.far)
+    g.wait_ge(sem.sent, n_sent)
+
+    S.wait_ge(sem.b1s, 1)
+    S.activation(col(T.s0), col(T.land, own + 1), A.Sqrt, bias=EPS, scale=1.0 / float(SUB) ** 3).then_inc(sem.es0, 1)
+    V.wait_ge(sem.es0, 1)
+    V.reciprocal(col(T.hh, 0), col(T.s0)).then_inc(sem.eis, 1)
+    V.wait_ge(sem.eis, 1)
+    for i, c in enumerate((SUB / float(NT) ** 3, 1.0 / (float(SUB) ** 2 * NT), EPS)):
+        V.tensor_scalar(col(T.kk, i), col(T.hh, 0), col(T.hh, 0), float(c), mult, mult).then_inc(sem.ek, 1)
+    V.wait_ge(sem.ek, 3)
+    for j in range(NS):
+        V.wait_ge(sem["a%d" % j], 1)
+    S.wait_ge(sem.ek, 3)
+    S.wait_ge(sem.b2s, NS - 1)
+
+    allA, allB = T.land[:, 0::2], T.land[:, 1::2]
+    V.wait_ge(sem.peer, n_peer)
+    V.wait_ge(sem.far, n_far)
+    S.wait_ge(sem.peer, n_peer)
+    S.wait_ge(sem.far, n_far)
+    V.tensor_reduce(col(T.r1), allA, AxisListType.X, add, negate=True).then_inc(sem.er1, 1)
+    S.activation(T.j1[:, :], allB, A.Copy, accum_out=col(T.ww)).then_inc(sem.ew, 1)
+    S.wait_ge(sem.er1, 1)
+    S.activation(T.j2[:, :], allA, A.Square, bias=col(T.r1), scale=float(KT),
+                 accum_out=col(T.qq)).then_inc(sem.eq, 1)
+    V.wait_ge(sem.ew, 1)
+    V.tensor_scalar(col(T.w2), col(T.ww), col(T.kk, 1), col(T.kk, 2), mult, add).then_inc(sem.ew2, 1)
+    S.wait_ge(sem.eq, 1)
+    S.wait_ge(sem.ew2, 1)
+    S.activation(col(T.tt), col(T.qq), A.Sqrt, bias=col(T.w2), scale=col(T.kk, 0)).then_inc(sem.et, 1)
+    V.wait_ge(sem.er1, 1)
+    V.tensor_scalar(col(T.mu), col(T.r1), 1.0 / NT, None, mult).then_inc(sem.emu, 1)
+    V.tensor_scalar(col(T.hh, 1), col(T.r1), -1.0 / NT, col(T.hh, 0), mult, mult).then_inc(sem.emu, 1)
+    V.wait_ge(sem.emu, 2)
+    V.wait_ge(sem.et, 1)
+    V.reciprocal(col(T.rt), col(T.tt)).then_inc(sem.ert, 1)
+    V.wait_ge(sem.ert, 1)
+    V.tensor_scalar(T.rn[:, 0:2], T.hh[:, 0:2], col(T.rt), None, mult).then_inc(sem.ers, 1)
+    V.wait_ge(sem.ers, 1)
+    S.wait_ge(sem.ers, 1)
+
+    for i, ((vl, vh), (sl, sh)) in enumerate(STORES):
+        V.tensor_scalar(T.ys[:, vl:vh], T.xs[:, vl:vh], col(T.mu), col(T.rn, 0), sub, mult).then_inc(sem["nv%d" % i], 1)
+        S.activation(T.ys[:, sl:sh], T.xs[:, sl:sh], A.Identity, bias=col(T.rn, 1),
+                     scale=col(T.rn, 0)).then_inc(sem["ns%d" % i], 1)
+        Y.wait_ge(sem["nv%d" % i], 1)
+        Y.wait_ge(sem["ns%d" % i], 1)
+        Y.dma_start(T.y[:, vl:sh], T.ys[:, vl:sh]).then_inc(sem.st, 16)
+    Y.wait_ge(sem.st, 16 * len(STORES))

@@ -5,20 +5,24 @@ NR = 9
 TK = 1024
 NT = NR * TK
 EPS = 0.01
-SUB = 128
-NS = TK // SUB
-KT = NR * NS
-SLOT = 2 * NS
-LOADS = [(0, 512), (512, 1024)]
-STORES = [((0, 128), (128, 256)), ((256, 640), (640, 1024))]
+SLOT = 4
+LOADS = [(0, 128), (128, 512), (512, 896), (896, 1024)]
+NB = len(LOADS)
+PRE = 192
 
 SCRATCH = {
     "xs": ("sbuf", [128, TK], "float32"),
     "ys": ("sbuf", [128, TK], "float32"),
     "sq": ("sbuf", [128, TK], "float32"),
+    "xc": ("sbuf", [128, PRE], "float32"),
     "land": ("sbuf", [128, NR * SLOT], "float32"),
-    "j1": ("sbuf", [128, KT], "float32"),
-    "j2": ("sbuf", [128, KT], "float32"),
+    "av": ("sbuf", [128, 4], "float32"),
+    "bv": ("sbuf", [128, 4], "float32"),
+    "np": ("sbuf", [128, 4], "float32"),
+    "gq": ("sbuf", [128, 4], "float32"),
+    "bs": ("sbuf", [128, 4], "float32"),
+    "j1": ("sbuf", [128, 2 * NR], "float32"),
+    "j2": ("sbuf", [128, 2 * NR], "float32"),
     "s0": ("sbuf", [128, 4], "float32"),
     "hh": ("sbuf", [128, 4], "float32"),
     "kk": ("sbuf", [128, 4], "float32"),
@@ -26,15 +30,13 @@ SCRATCH = {
     "ww": ("sbuf", [128, 4], "float32"),
     "qq": ("sbuf", [128, 4], "float32"),
     "w2": ("sbuf", [128, 4], "float32"),
-    "mu": ("sbuf", [128, 4], "float32"),
     "tt": ("sbuf", [128, 4], "float32"),
     "rt": ("sbuf", [128, 4], "float32"),
     "rn": ("sbuf", [128, 4], "float32"),
 }
-SEMAPHORES = (["ld%d" % i for i in range(len(LOADS))] + ["a%d" % j for j in range(NS)]
-              + ["b1s", "b2s", "peer", "far", "sent", "es0", "eis", "ek", "er1", "ew", "eq", "ew2", "emu", "et",
-                 "ert", "ers", "st"]
-              + ["nv%d" % i for i in range(len(STORES))] + ["ns%d" % i for i in range(len(STORES))])
+SEMAPHORES = (["ld%d" % i for i in range(NB)]
+              + ["ez", "enp", "ea", "b1s", "eb", "es1", "eg", "ebs", "eb2", "peer", "far", "sent", "es0", "eis", "ek",
+                 "er1", "ew", "eq", "ew2", "eh", "et", "exc", "ert", "ers", "n0", "n1", "n2", "st"])
 
 
 def _bits(m):
@@ -84,6 +86,7 @@ def rank_program(g, core, T, topo):
     sem = T.sem
     A = ActivationFunctionType
     mult, add, sub = AluOpType.mult, AluOpType.add, AluOpType.subtract
+    X = AxisListType.X
     groups, slot, serve = _plan(list(T.cores), topo)
     mine = [grp for grp in groups if core in grp][0]
     peers = [c for c in mine if c != core]
@@ -96,82 +99,94 @@ def rank_program(g, core, T, topo):
         return t[:, i:i + 1]
 
     for i, (lo, hi) in enumerate(LOADS):
-        (Y if i % 2 == 0 else S).dma_start(T.xs[:, lo:hi], T.x[:, lo:hi]).then_inc(sem["ld%d" % i], 16)
+        Y.dma_start(T.xs[:, lo:hi], T.x[:, lo:hi]).then_inc(sem["ld%d" % i], 16)
 
-    seen_v, seen_s = -1, -1
-    for j in range(NS):
-        lo, hi = j * SUB, (j + 1) * SUB
-        blk = [i for i, (a, b) in enumerate(LOADS) if a <= lo and hi <= b][0]
-        if blk != seen_v:
-            V.wait_ge(sem["ld%d" % blk], 16)
-            seen_v = blk
-        V.tensor_reduce(col(T.land, own + 2 * j), T.xs[:, lo:hi], AxisListType.X, add,
-                        negate=True).then_inc(sem["a%d" % j], 1)
-    for j in range(NS):
-        lo, hi = j * SUB, (j + 1) * SUB
-        blk = [i for i, (a, b) in enumerate(LOADS) if a <= lo and hi <= b][0]
-        if blk != seen_s:
-            S.wait_ge(sem["ld%d" % blk], 16)
-            seen_s = blk
-        S.wait_ge(sem["a%d" % j], 1)
-        S.activation(T.sq[:, lo:hi], T.xs[:, lo:hi], A.Square, bias=col(T.land, own + 2 * j), scale=float(SUB),
-                     accum_out=col(T.land, own + 2 * j + 1)).then_inc(sem.b1s if j == 0 else sem.b2s, 1)
+    V.memset(col(T.land, own + 3), 0.0).then_inc(sem.ez, 1)
+    for i, (lo, hi) in enumerate(LOADS):
+        V.wait_ge(sem["ld%d" % i], 16)
+        V.tensor_reduce(col(T.av, i), T.xs[:, lo:hi], X, add).then_inc(sem.ea, 1)
+        if i == 0:
+            V.tensor_scalar(col(T.np), col(T.xs, 0), -32.0, None, mult).then_inc(sem.enp, 1)
+        S.wait_ge(sem["ld%d" % i], 16)
+        S.activation(T.sq[:, lo:hi], T.xs[:, lo:hi], A.Square, bias=col(T.xs, 0), scale=-1.0,
+                     accum_out=col(T.land, own) if i == 0 else col(T.bv, i)).then_inc(sem.b1s if i == 0 else sem.eb, 1)
+    V.wait_ge(sem.ea, NB)
+    V.tensor_reduce(col(T.land, own + 1), T.av[:, 0:NB], X, add).then_inc(sem.es1, 1)
+    S.wait_ge(sem.enp, 1)
+    S.wait_ge(sem.es1, 1)
+    S.activation(col(T.gq), col(T.land, own + 1), A.Square, bias=col(T.np), scale=1.0 / 32.0).then_inc(sem.eg, 1)
+    V.wait_ge(sem.eb, NB - 1)
+    V.tensor_reduce(col(T.bs), T.bv[:, 1:NB], X, add).then_inc(sem.ebs, 1)
+    V.wait_ge(sem.ebs, 1)
+    V.wait_ge(sem.eg, 1)
+    V.tensor_scalar(col(T.land, own + 2), col(T.bs), col(T.gq), None, sub).then_inc(sem.eb2, 1)
 
     n_sent = 0
-    g.wait_ge(sem.a0, 1)
     g.wait_ge(sem.b1s, 1)
-    n_sent += _send(g, T, topo, core, peers, own, own + 2, sem.peer)
-    g.wait_ge(sem.b2s, NS - 1)
-    n_sent += _send(g, T, topo, core, peers, own + 2, own + SLOT, sem.peer)
+    n_sent += _send(g, T, topo, core, peers, own, own + 1, sem.peer)
+    g.wait_ge(sem.ez, 1)
+    g.wait_ge(sem.es1, 1)
+    g.wait_ge(sem.eb2, 1)
+    n_sent += _send(g, T, topo, core, peers, own + 1, own + SLOT, sem.peer)
     g.wait_ge(sem.peer, n_peer)
     if serve[core]:
         n_sent += _send(g, T, topo, core, serve[core], blk_lo, blk_hi, sem.far)
     g.wait_ge(sem.sent, n_sent)
 
     S.wait_ge(sem.b1s, 1)
-    S.activation(col(T.s0), col(T.land, own + 1), A.Sqrt, bias=EPS, scale=1.0 / float(SUB) ** 3).then_inc(sem.es0, 1)
+    S.activation(col(T.s0), col(T.land, own), A.Sqrt, bias=EPS,
+                 scale=1.0 / (LOADS[0][1] - LOADS[0][0])).then_inc(sem.es0, 1)
     V.wait_ge(sem.es0, 1)
     V.reciprocal(col(T.hh, 0), col(T.s0)).then_inc(sem.eis, 1)
     V.wait_ge(sem.eis, 1)
-    for i, c in enumerate((SUB / float(NT) ** 3, 1.0 / (float(SUB) ** 2 * NT), EPS)):
+    for i, c in enumerate((1.0 / (float(NR * NR) * TK * NT), 1.0 / NT, EPS)):
         V.tensor_scalar(col(T.kk, i), col(T.hh, 0), col(T.hh, 0), float(c), mult, mult).then_inc(sem.ek, 1)
     V.wait_ge(sem.ek, 3)
-    for j in range(NS):
-        V.wait_ge(sem["a%d" % j], 1)
+    V.wait_ge(sem.eb2, 1)
+    V.wait_ge(sem.es1, 1)
+    V.wait_ge(sem.ez, 1)
+    S.wait_ge(sem.eis, 1)
     S.wait_ge(sem.ek, 3)
-    S.wait_ge(sem.b2s, NS - 1)
+    S.wait_ge(sem.eb2, 1)
 
-    allA, allB = T.land[:, 0::2], T.land[:, 1::2]
+    allA, allB = T.land[:, 1::SLOT], T.land[:, 0::2]
     V.wait_ge(sem.peer, n_peer)
     V.wait_ge(sem.far, n_far)
     S.wait_ge(sem.peer, n_peer)
     S.wait_ge(sem.far, n_far)
-    V.tensor_reduce(col(T.r1), allA, AxisListType.X, add, negate=True).then_inc(sem.er1, 1)
+    V.tensor_reduce(col(T.r1), allA, X, add, negate=True).then_inc(sem.er1, 1)
     S.activation(T.j1[:, :], allB, A.Copy, accum_out=col(T.ww)).then_inc(sem.ew, 1)
     S.wait_ge(sem.er1, 1)
-    S.activation(T.j2[:, :], allA, A.Square, bias=col(T.r1), scale=float(KT),
+    S.activation(T.j2[:, 0:NR], allA, A.Square, bias=col(T.r1), scale=float(NR),
                  accum_out=col(T.qq)).then_inc(sem.eq, 1)
     V.wait_ge(sem.ew, 1)
     V.tensor_scalar(col(T.w2), col(T.ww), col(T.kk, 1), col(T.kk, 2), mult, add).then_inc(sem.ew2, 1)
+    V.wait_ge(sem.er1, 1)
+    V.tensor_scalar(col(T.hh, 1), col(T.r1), 1.0 / NT, col(T.hh, 0), mult, mult).then_inc(sem.eh, 1)
     S.wait_ge(sem.eq, 1)
     S.wait_ge(sem.ew2, 1)
     S.activation(col(T.tt), col(T.qq), A.Sqrt, bias=col(T.w2), scale=col(T.kk, 0)).then_inc(sem.et, 1)
-    V.wait_ge(sem.er1, 1)
-    V.tensor_scalar(col(T.mu), col(T.r1), 1.0 / NT, None, mult).then_inc(sem.emu, 1)
-    V.tensor_scalar(col(T.hh, 1), col(T.r1), -1.0 / NT, col(T.hh, 0), mult, mult).then_inc(sem.emu, 1)
-    V.wait_ge(sem.emu, 2)
     V.wait_ge(sem.et, 1)
     V.reciprocal(col(T.rt), col(T.tt)).then_inc(sem.ert, 1)
+    S.wait_ge(sem.eh, 1)
+    S.activation(T.xc[:, :], T.xs[:, 0:PRE], A.Identity, bias=col(T.hh, 1), scale=col(T.hh, 0)).then_inc(sem.exc, 1)
+
     V.wait_ge(sem.ert, 1)
+    V.wait_ge(sem.exc, 1)
+    V.wait_ge(sem.eh, 1)
+    S.wait_ge(sem.ert, 1)
+    S.wait_ge(sem.exc, 1)
+    V.tensor_scalar(T.ys[:, 0:64], T.xc[:, 0:64], col(T.rt), None, mult).then_inc(sem.n0, 1)
+    S.activation(T.ys[:, 64:128], T.xc[:, 64:128], A.Identity, scale=col(T.rt)).then_inc(sem.n0, 1)
     V.tensor_scalar(T.rn[:, 0:2], T.hh[:, 0:2], col(T.rt), None, mult).then_inc(sem.ers, 1)
+    S.activation(T.ys[:, 128:PRE], T.xc[:, 128:PRE], A.Identity, scale=col(T.rt)).then_inc(sem.n1, 1)
     V.wait_ge(sem.ers, 1)
     S.wait_ge(sem.ers, 1)
-
-    for i, ((vl, vh), (sl, sh)) in enumerate(STORES):
-        V.tensor_scalar(T.ys[:, vl:vh], T.xs[:, vl:vh], col(T.mu), col(T.rn, 0), sub, mult).then_inc(sem["nv%d" % i], 1)
+    for name, (vl, vh), (sl, sh) in (("n1", (PRE, 352), (352, 512)), ("n2", (512, 768), (768, 1024))):
+        V.tensor_scalar(T.ys[:, vl:vh], T.xs[:, vl:vh], col(T.rn, 0), col(T.rn, 1), mult, add).then_inc(sem[name], 1)
         S.activation(T.ys[:, sl:sh], T.xs[:, sl:sh], A.Identity, bias=col(T.rn, 1),
-                     scale=col(T.rn, 0)).then_inc(sem["ns%d" % i], 1)
-        Y.wait_ge(sem["nv%d" % i], 1)
-        Y.wait_ge(sem["ns%d" % i], 1)
-        Y.dma_start(T.y[:, vl:sh], T.ys[:, vl:sh]).then_inc(sem.st, 16)
-    Y.wait_ge(sem.st, 16 * len(STORES))
+                     scale=col(T.rn, 0)).then_inc(sem[name], 1)
+    for name, n, lo, hi in (("n0", 2, 0, 128), ("n1", 3, 128, 512), ("n2", 2, 512, 1024)):
+        Y.wait_ge(sem[name], n)
+        Y.dma_start(T.y[:, lo:hi], T.ys[:, lo:hi]).then_inc(sem.st, 16)
+    Y.wait_ge(sem.st, 48)

from concourse.bass import DstId, RemoteDMATransfer
from concourse.mybir import AluOpType, AxisListType, ActivationFunctionType

NR = 9
TK = 1024
NT = NR * TK
EPS = 0.01
SLOT = 4
LOADS = [(0, 128), (128, 512), (512, 896), (896, 1024)]
NB = len(LOADS)
PRE = 192

SCRATCH = {
    "xs": ("sbuf", [128, TK], "float32"),
    "ys": ("sbuf", [128, TK], "float32"),
    "sq": ("sbuf", [128, TK], "float32"),
    "xc": ("sbuf", [128, PRE], "float32"),
    "land": ("sbuf", [128, NR * SLOT], "float32"),
    "av": ("sbuf", [128, 4], "float32"),
    "bv": ("sbuf", [128, 4], "float32"),
    "np": ("sbuf", [128, 4], "float32"),
    "gq": ("sbuf", [128, 4], "float32"),
    "bs": ("sbuf", [128, 4], "float32"),
    "j1": ("sbuf", [128, 2 * NR], "float32"),
    "j2": ("sbuf", [128, 2 * NR], "float32"),
    "s0": ("sbuf", [128, 4], "float32"),
    "hh": ("sbuf", [128, 4], "float32"),
    "kk": ("sbuf", [128, 4], "float32"),
    "r1": ("sbuf", [128, 4], "float32"),
    "ww": ("sbuf", [128, 4], "float32"),
    "qq": ("sbuf", [128, 4], "float32"),
    "w2": ("sbuf", [128, 4], "float32"),
    "tt": ("sbuf", [128, 4], "float32"),
    "rt": ("sbuf", [128, 4], "float32"),
    "rn": ("sbuf", [128, 4], "float32"),
}
SEMAPHORES = (["ld%d" % i for i in range(NB)]
              + ["ez", "enp", "ea", "b1s", "eb", "es1", "eg", "ebs", "eb2", "peer", "far", "sent", "es0", "eis", "ek",
                 "er1", "ew", "eq", "ew2", "eh", "et", "exc", "ert", "ers", "n0", "n1", "n2", "st"])


def _bits(m):
    return bin(m).count("1")


def _plan(cores, topo):
    chips = []
    for c in cores:
        if topo.chip(c) not in chips:
            chips.append(topo.chip(c))
    groups = [[c for c in cores if topo.chip(c) == ch] for ch in chips]
    slot = {}
    for grp in groups:
        for c in grp:
            slot[c] = len(slot)
    serve = {c: [] for c in cores}
    for grp in groups:
        dests = [d for d in cores if d not in grp]
        can = {d: [s for s in grp if topo.may_write(s, d)] for d in dests}
        for d in sorted(dests, key=lambda d: (len(can[d]), slot[d])):
            s = min(can[d], key=lambda s: (len(serve[s]), 0 if topo.die(s) == topo.die(d) else 1, slot[s]))
            serve[s].append(d)
    return groups, slot, serve


def _mask(core, dests, topo):
    m = topo.mask(core, dests[0])
    for d in dests[1:]:
        m &= topo.mask(core, d)
    return m


def _send(g, T, topo, core, dests, lo, hi, sem):
    m = _mask(core, dests, topo)
    ids = [DstId(rid=topo.addr(d)[0], pnc=topo.addr(d)[1]) for d in dests]
    g.remote_dma_fused([RemoteDMATransfer(dst_ids=ids, dma_engine_mask=m, remote_sem=sem,
                                          srcs=[T.land[:, lo:hi]], dsts=[T.land[:, lo:hi] for d in dests],
                                          alu_op=0)], local_sem=T.sem.sent)
    return _bits(m)


def rank_program(g, core, T, topo):
    if T.rank_of(core) is None:
        return
    V, S, Y = g.vector, g.scalar, g.sync
    sem = T.sem
    A = ActivationFunctionType
    mult, add, sub = AluOpType.mult, AluOpType.add, AluOpType.subtract
    X = AxisListType.X
    groups, slot, serve = _plan(list(T.cores), topo)
    mine = [grp for grp in groups if core in grp][0]
    peers = [c for c in mine if c != core]
    own = slot[core] * SLOT
    blk_lo, blk_hi = slot[mine[0]] * SLOT, (slot[mine[-1]] + 1) * SLOT
    n_peer = sum(2 * _bits(_mask(p, [c for c in mine if c != p], topo)) for p in peers)
    n_far = sum(_bits(_mask(s, serve[s], topo)) for s in T.cores if core in serve[s])

    def col(t, i=0):
        return t[:, i:i + 1]

    for i, (lo, hi) in enumerate(LOADS):
        Y.dma_start(T.xs[:, lo:hi], T.x[:, lo:hi]).then_inc(sem["ld%d" % i], 16)

    V.memset(col(T.land, own + 3), 0.0).then_inc(sem.ez, 1)
    for i, (lo, hi) in enumerate(LOADS):
        V.wait_ge(sem["ld%d" % i], 16)
        V.tensor_reduce(col(T.av, i), T.xs[:, lo:hi], X, add).then_inc(sem.ea, 1)
        if i == 0:
            V.tensor_scalar(col(T.np), col(T.xs, 0), -32.0, None, mult).then_inc(sem.enp, 1)
        S.wait_ge(sem["ld%d" % i], 16)
        S.activation(T.sq[:, lo:hi], T.xs[:, lo:hi], A.Square, bias=col(T.xs, 0), scale=-1.0,
                     accum_out=col(T.land, own) if i == 0 else col(T.bv, i)).then_inc(sem.b1s if i == 0 else sem.eb, 1)
    V.wait_ge(sem.ea, NB)
    V.tensor_reduce(col(T.land, own + 1), T.av[:, 0:NB], X, add).then_inc(sem.es1, 1)
    S.wait_ge(sem.enp, 1)
    S.wait_ge(sem.es1, 1)
    S.activation(col(T.gq), col(T.land, own + 1), A.Square, bias=col(T.np), scale=1.0 / 32.0).then_inc(sem.eg, 1)
    V.wait_ge(sem.eb, NB - 1)
    V.tensor_reduce(col(T.bs), T.bv[:, 1:NB], X, add).then_inc(sem.ebs, 1)
    V.wait_ge(sem.ebs, 1)
    V.wait_ge(sem.eg, 1)
    V.tensor_scalar(col(T.land, own + 2), col(T.bs), col(T.gq), None, sub).then_inc(sem.eb2, 1)

    n_sent = 0
    g.wait_ge(sem.b1s, 1)
    n_sent += _send(g, T, topo, core, peers, own, own + 1, sem.peer)
    g.wait_ge(sem.ez, 1)
    g.wait_ge(sem.es1, 1)
    g.wait_ge(sem.eb2, 1)
    n_sent += _send(g, T, topo, core, peers, own + 1, own + SLOT, sem.peer)
    g.wait_ge(sem.peer, n_peer)
    if serve[core]:
        n_sent += _send(g, T, topo, core, serve[core], blk_lo, blk_hi, sem.far)
    g.wait_ge(sem.sent, n_sent)

    S.wait_ge(sem.b1s, 1)
    S.activation(col(T.s0), col(T.land, own), A.Sqrt, bias=EPS,
                 scale=1.0 / (LOADS[0][1] - LOADS[0][0])).then_inc(sem.es0, 1)
    V.wait_ge(sem.es0, 1)
    V.reciprocal(col(T.hh, 0), col(T.s0)).then_inc(sem.eis, 1)
    V.wait_ge(sem.eis, 1)
    for i, c in enumerate((1.0 / (float(NR * NR) * TK * NT), 1.0 / NT, EPS)):
        V.tensor_scalar(col(T.kk, i), col(T.hh, 0), col(T.hh, 0), float(c), mult, mult).then_inc(sem.ek, 1)
    V.wait_ge(sem.ek, 3)
    V.wait_ge(sem.eb2, 1)
    V.wait_ge(sem.es1, 1)
    V.wait_ge(sem.ez, 1)
    S.wait_ge(sem.eis, 1)
    S.wait_ge(sem.ek, 3)
    S.wait_ge(sem.eb2, 1)

    allA, allB = T.land[:, 1::SLOT], T.land[:, 0::2]
    V.wait_ge(sem.peer, n_peer)
    V.wait_ge(sem.far, n_far)
    S.wait_ge(sem.peer, n_peer)
    S.wait_ge(sem.far, n_far)
    V.tensor_reduce(col(T.r1), allA, X, add, negate=True).then_inc(sem.er1, 1)
    S.activation(T.j1[:, :], allB, A.Copy, accum_out=col(T.ww)).then_inc(sem.ew, 1)
    S.wait_ge(sem.er1, 1)
    S.activation(T.j2[:, 0:NR], allA, A.Square, bias=col(T.r1), scale=float(NR),
                 accum_out=col(T.qq)).then_inc(sem.eq, 1)
    V.wait_ge(sem.ew, 1)
    V.tensor_scalar(col(T.w2), col(T.ww), col(T.kk, 1), col(T.kk, 2), mult, add).then_inc(sem.ew2, 1)
    V.wait_ge(sem.er1, 1)
    V.tensor_scalar(col(T.hh, 1), col(T.r1), 1.0 / NT, col(T.hh, 0), mult, mult).then_inc(sem.eh, 1)
    S.wait_ge(sem.eq, 1)
    S.wait_ge(sem.ew2, 1)
    S.activation(col(T.tt), col(T.qq), A.Sqrt, bias=col(T.w2), scale=col(T.kk, 0)).then_inc(sem.et, 1)
    V.wait_ge(sem.et, 1)
    V.reciprocal(col(T.rt), col(T.tt)).then_inc(sem.ert, 1)
    S.wait_ge(sem.eh, 1)
    S.activation(T.xc[:, :], T.xs[:, 0:PRE], A.Identity, bias=col(T.hh, 1), scale=col(T.hh, 0)).then_inc(sem.exc, 1)

    V.wait_ge(sem.ert, 1)
    V.wait_ge(sem.exc, 1)
    V.wait_ge(sem.eh, 1)
    S.wait_ge(sem.ert, 1)
    S.wait_ge(sem.exc, 1)
    V.tensor_scalar(T.ys[:, 0:64], T.xc[:, 0:64], col(T.rt), None, mult).then_inc(sem.n0, 1)
    S.activation(T.ys[:, 64:128], T.xc[:, 64:128], A.Identity, scale=col(T.rt)).then_inc(sem.n0, 1)
    V.tensor_scalar(T.rn[:, 0:2], T.hh[:, 0:2], col(T.rt), None, mult).then_inc(sem.ers, 1)
    S.activation(T.ys[:, 128:PRE], T.xc[:, 128:PRE], A.Identity, scale=col(T.rt)).then_inc(sem.n1, 1)
    V.wait_ge(sem.ers, 1)
    S.wait_ge(sem.ers, 1)
    for name, (vl, vh), (sl, sh) in (("n1", (PRE, 352), (352, 512)), ("n2", (512, 768), (768, 1024))):
        V.tensor_scalar(T.ys[:, vl:vh], T.xs[:, vl:vh], col(T.rn, 0), col(T.rn, 1), mult, add).then_inc(sem[name], 1)
        S.activation(T.ys[:, sl:sh], T.xs[:, sl:sh], A.Identity, bias=col(T.rn, 1),
                     scale=col(T.rn, 0)).then_inc(sem[name], 1)
    for name, n, lo, hi in (("n0", 2, 0, 128), ("n1", 3, 128, 512), ("n2", 2, 512, 1024)):
        Y.wait_ge(sem[name], n)
        Y.dma_start(T.y[:, lo:hi], T.ys[:, lo:hi]).then_inc(sem.st, 16)
    Y.wait_ge(sem.st, 48)
